import numpy as np
import ml_dtypes


def mxq(x, axis, fmt="e4m3"):
    dtype, down = {"e4m3": (ml_dtypes.float8_e4m3fn, 7), "e5m2": (ml_dtypes.float8_e5m2, 14)}[fmt]
    v = np.moveaxis(np.asarray(x, np.float32).astype(ml_dtypes.bfloat16).astype(np.float64), axis, -1)
    blocks = v.reshape(v.shape[:-1] + (-1, 32))
    amax = np.abs(blocks).max(-1, keepdims=True)
    byte = np.maximum(np.where(amax > 0, np.frexp(amax)[1] - 1 + 127, 0) - down, 1)
    scale = np.exp2(byte - 127.0)
    codes = (blocks / scale).astype(np.float32).astype(dtype).astype(np.float64)
    return np.moveaxis((codes * scale).reshape(v.shape), -1, axis)


WIDE = False


def mx_kscale(k):
    if not WIDE:
        return np.ones(k)
    levels = np.array([10, -10, 5, -5, 0])
    if k % 512:
        return np.exp2(np.random.permutation(np.resize(levels, k // 32))).repeat(32)
    a = np.empty((k // 512, 16))
    for p in range(k // 512):
        a[p, :8] = np.random.permutation(np.resize(levels, 8))
        for g in range(8):
            far = levels[np.abs(levels - a[p, g]) >= 10]
            a[p, g + 8] = far[np.random.randint(len(far))]
    return np.exp2(a.ravel()).repeat(32)


def f64(x):
    return np.asarray(x).astype(np.float64)


def striped(idx):
    return np.tile(idx.reshape(-1, 16).T, (8, 1)).astype(np.uint16)


def unstriped(offs):
    return offs[:16].T.reshape(-1).astype(np.int64)


E2M1 = np.array([0.0, 0.5, 1.0, 1.5, 2.0, 3.0, 4.0, 6.0, -0.0, -0.5, -1.0, -1.5, -2.0, -3.0, -4.0, -6.0])


def pack_weight(w, fmt):
    k, n = w.shape
    w = f64(np.asarray(w, np.float32).astype(ml_dtypes.bfloat16)).reshape(k // 32, 32, n)
    amax = np.abs(w).max(1)
    if fmt == "e4m3":
        byte = np.frexp(amax)[1] - 1 + 127 - 7
    else:
        mant, ex = np.frexp(amax / 6.0)
        byte = np.where(mant > 0.5, ex, ex - 1) + 127
    byte = np.clip(np.where(amax > 0, byte, 1), 1, 254)
    scaled = (w * np.exp2(127.0 - byte)[:, None, :]).reshape(k, n).astype(np.float32)
    by_word = np.ascontiguousarray(scaled.reshape(k // 512, 128, 4, n).transpose(0, 1, 3, 2))
    if fmt == "e4m3":
        words = by_word.astype(ml_dtypes.float8_e4m3fn).view(np.uint8)
    else:
        c = by_word.astype(ml_dtypes.float4_e2m1fn).view(np.uint8) & 0xF
        words = (c[..., 0::2] | (c[..., 1::2] << 4)).reshape(k // 512, 128, 2 * n)
    return np.ascontiguousarray(words), np.ascontiguousarray(byte.astype(np.uint8).reshape(k // 512, 16, n))


def unpack_weight(words, scales, fmt):
    g, _, n = scales.shape
    words = np.ascontiguousarray(words).reshape(g, 128, n, -1)
    if fmt == "e4m3":
        vals = words.view(ml_dtypes.float8_e4m3fn).astype(np.float64)
    else:
        nib = np.empty((g, 128, n, 4), np.uint8)
        nib[..., 0::2] = words & 0xF
        nib[..., 1::2] = words >> 4
        vals = E2M1[nib]
    vals = vals * np.repeat(np.exp2(scales.astype(np.float64) - 127.0), 8, axis=1)[..., None]
    return vals.transpose(0, 1, 3, 2).reshape(g * 512, n)


def gelu(v):
    return 0.5 * v * (1.0 + np.tanh(np.sqrt(2.0 / np.pi) * (v + 0.044715 * v**3)))


K, KA, KB, H, T, S, T3, S2 = 1536, 1024, 512, 1024, 2048, 512, 2048, 512


def setup_inputs():
    n = np.random.standard_normal
    s = mx_kscale(K)[:, None]
    u = mx_kscale(H)[:, None]
    tab_words, tab_scales = pack_weight(n((K, T)) * s, "e4m3")
    tab2_words, tab2_scales = pack_weight(n((H, T3)) / np.sqrt(H) / u, "e4m3")
    tab3_words, tab3_scales = pack_weight(1.4 * n((H, T3)) / np.sqrt(H) / u, "e4m3")
    w1 = 1.3 * n((KA, H)) / np.sqrt(K) / s[:KA]
    w4_words, w4_scales = pack_weight(1.3 * n((KB, H)) / np.sqrt(K) / s[KA:], "e2m1")
    return {"tab_words": tab_words, "tab_scales": tab_scales,
            "offs": striped(np.random.permutation(T)[:S]),
            "w1": w1.astype(np.float32),
            "w4_words": w4_words, "w4_scales": w4_scales,
            "gain": (np.exp(0.3 * n(H)) * u[:, 0]).astype(np.float32),
            "res": (0.6 * n((H, S)) * u).astype(np.float32),
            "tab2_words": tab2_words, "tab2_scales": tab2_scales,
            "offs2": striped(np.random.permutation(T3)[:S2]),
            "tab3_words": tab3_words, "tab3_scales": tab3_scales,
            "offs3": striped(np.random.permutation(T3)[:S2])}


def reference(tab_words, tab_scales, offs, w1, w4_words, w4_scales, gain, res,
              tab2_words, tab2_scales, offs2, tab3_words, tab3_scales, offs3):
    v = unpack_weight(tab_words, tab_scales, "e4m3")[:, unstriped(offs)]
    v2 = unpack_weight(tab2_words, tab2_scales, "e4m3")[:, unstriped(offs2)]
    v3 = unpack_weight(tab3_words, tab3_scales, "e4m3")[:, unstriped(offs3)]
    w1q = mxq(f64(w1), 0, "e4m3")
    w4 = unpack_weight(w4_words, w4_scales, "e2m1")
    d = w1q.T @ v[:KA] + w4.T @ v[KA:]
    h = f64(gain)[:, None] * np.tanh(d) + f64(res)
    hq = mxq(h, 0, "e4m3")
    e2 = v2.T @ hq
    e3 = v3.T @ hq
    return e2 * np.tanh(e3) + np.abs(e2)

@@ -1,0 +1,261 @@
+from contextlib import ExitStack
+from functools import partial
+
+import concourse.mybir as mybir
+
+K, KA, KB, H, T, S = 1536, 1024, 512, 1024, 2048, 512
+FLOPS = 2 * K * H * S + 2 * 2 * H * S * S
+
+F32 = mybir.dt.float32
+BF16 = mybir.dt.bfloat16
+I32 = mybir.dt.int32
+U32 = mybir.dt.uint32
+U16 = mybir.dt.uint16
+U8 = mybir.dt.uint8
+FP8X4 = mybir.dt.float8_e4m3fn_x4
+FP4X4 = mybir.dt.float4_e2m1fn_x4
+ACT = mybir.ActivationFunctionType
+ALU = mybir.AluOpType
+
+P = 128
+PACK = 4
+K_PASS = P * PACK
+QUADS = 4
+QUAD = P // QUADS
+H_PASSES = H // K_PASS
+W1_PASSES = KA // K_PASS
+M_TILES = S // P
+LIST_COLS = S // 16
+NEAR = 4
+
+
+def tile_list_board_longlist_readout_kernel(
+    tc, tab_words, tab_scales, offs, w1, w4_words, w4_scales, gain, res,
+    tab2_words, tab2_scales, offs2, tab3_words, tab3_scales, offs3, out,
+):
+    nc = tc.nc
+    with ExitStack() as ctx:
+        keep = ctx.enter_context(tc.tile_pool(name="keep", bufs=1))
+        psum = ctx.enter_context(tc.psum_pool(name="psum", bufs=1))
+
+        def sb(name, shape, dtype, reuse=None):
+            return keep.tile(shape, dtype, name=name, tag=reuse or name, align_bytes=64)
+
+        def bank(index):
+            return psum.tile([P, S], F32, name="bank%d" % index)
+
+        lists = [sb("list%d" % i, [P, LIST_COLS], U16) for i in range(3)]
+        tab_win = [sb("tab_win%d" % a, [P, T], I32) for a in range(3)]
+        tab2_win = [sb("tab2_win%d" % a, [P, T], I32) for a in range(H_PASSES)]
+        tab3_win = [sb("tab3_win%d" % a, [P, T], I32) for a in range(H_PASSES)]
+        scale_win = [sb("scale_win%d" % i, [P, T], U8) for i in range(3)]
+        w4_raw = sb("w4_raw", [P, 2 * H], U8)
+        w4_scale_raw = sb("w4_scale_raw", [P, H], U8)
+        w1_raw = {(a, b): sb("w1_raw%d%d" % (a, b), [P, PACK, K_PASS], F32)
+                  for a in range(W1_PASSES) for b in range(H_PASSES)}
+        res_sb = [sb("res%d" % b, [P, PACK, S], F32) for b in range(H_PASSES)]
+        gain_sb = sb("gain_sb", [P, H_PASSES, PACK], F32)
+
+        for plane in (scale_win[0], w4_scale_raw, scale_win[1], scale_win[2]):
+            nc.vector.memset(plane[:].bitcast(I32), 0)
+
+        def scale_loads(engine, plane, first_row, scales):
+            rows = scales.shape[0] * PACK
+
+            def load(q):
+                p0 = QUAD * q + first_row
+                engine.dma_start(
+                    out=plane[p0 : p0 + rows, :].bitcast(I32),
+                    in_=scales[:, PACK * q : PACK * (q + 1), :].bitcast(I32),
+                )
+
+            return [partial(load, q) for q in range(QUADS)]
+
+        tab_row = (4, 8, 0)
+        tab2_row = (0, 4)
+        tab3_row = (8, 12)
+
+        def load_words(win, words):
+            nc.sync.dma_start(out=win[:], in_=words.rearrange("p t i -> p (t i)").bitcast(I32))
+
+        def load_w1(a, b):
+            rows = w1[a * K_PASS : (a + 1) * K_PASS, b * K_PASS : (b + 1) * K_PASS]
+            nc.sync.dma_start(out=w1_raw[a, b][:], in_=rows.rearrange("(p j) c -> p j c", j=PACK))
+
+        def load_res(b):
+            rows = res[b * K_PASS : (b + 1) * K_PASS, :]
+            nc.sync.dma_start(out=res_sb[b][:], in_=rows.rearrange("(p t) j -> p t j", t=PACK))
+
+        def load_w4():
+            nc.sync.dma_start(out=w4_raw[:].bitcast(I32), in_=w4_words[0].bitcast(I32))
+
+        def load_gain():
+            nc.sync.dma_start(out=gain_sb[:], in_=gain.rearrange("(b p t) -> p b t", p=P, t=PACK))
+
+        def load_list(i, offsets):
+            nc.sync.dma_start(lists[i][:], offsets)
+
+        large = [
+            partial(load_w1, 0, 0), partial(load_words, tab_win[0], tab_words[0]),
+            partial(load_w1, 1, 0), partial(load_words, tab_win[1], tab_words[1]),
+            partial(load_w1, 0, 1), partial(load_words, tab_win[2], tab_words[2]),
+            partial(load_w1, 1, 1), partial(load_res, 0), partial(load_res, 1),
+        ]
+        large.extend(partial(load_words, tab2_win[a], tab2_words[a]) for a in range(H_PASSES))
+        large.extend(partial(load_words, tab3_win[a], tab3_words[a]) for a in range(H_PASSES))
+        small = [partial(load_list, 0, offs)]
+        small.extend(scale_loads(nc.sync, scale_win[0], tab_row[0], tab_scales[0:W1_PASSES]))
+        small.extend(scale_loads(nc.sync, scale_win[0], tab_row[2], tab_scales[W1_PASSES : W1_PASSES + 1]))
+        small.append(load_w4)
+        small.extend(scale_loads(nc.sync, w4_scale_raw, 0, w4_scales))
+        small.append(partial(load_list, 1, offs2))
+        small.extend(scale_loads(nc.sync, scale_win[1], tab2_row[0], tab2_scales))
+        small.extend([load_gain, partial(load_list, 2, offs3)])
+        small.extend(scale_loads(nc.sync, scale_win[2], tab3_row[0], tab3_scales))
+        large[0]()
+        for i, load in enumerate(large[1:]):
+            load()
+            first = 0 if i == 0 else 3 * (i + 1)
+            for small_load in small[first : 3 * (i + 2)]:
+                small_load()
+
+        def gather_words(name, win, offsets, pieces=1):
+            picked = sb(name, [P, S], U32)
+            width = S // pieces
+            for i in range(pieces):
+                piece = offsets[:, i * width // 16 : (i + 1) * width // 16]
+                nc.vector.tensor_copy(picked[:, i * width : (i + 1) * width], win[:].bitcast(U32).indirect(piece))
+            return picked
+
+        def gather_scales(name, win, offsets, reuse=None):
+            picked = sb(name, [P, S], U8, reuse)
+            nc.vector.tensor_copy(picked[:], win[:].indirect(offsets[:]))
+            return picked
+
+        def round_w1(a, b, scalar_share):
+            grouped = sb("w1_bf%d%d" % (a, b), [P, PACK * K_PASS], BF16)
+            dst = grouped[:].rearrange("p (t m j) -> p m j t", t=PACK, j=PACK)
+            src = w1_raw[a, b][:].rearrange("p j (m t) -> p m j t", t=PACK)
+            if scalar_share > 0:
+                nc.scalar.copy(dst[:, :scalar_share], src[:, :scalar_share])
+            if scalar_share < P:
+                nc.vector.tensor_copy(dst[:, scalar_share:], src[:, scalar_share:])
+            return grouped
+
+        def quantize(name, grouped, reuse=None):
+            codes = sb(name + "_codes", [P, K_PASS], U32, reuse)
+            scales = sb(name + "_scales", [P, K_PASS], U8)
+            nc.vector.quantize_mx(out=codes[:].bitcast(FP8X4), scales=scales[:], in_=grouped[:])
+            return codes, scales
+
+        sums = [bank(i) for i in range(H_PASSES * PACK)]
+        w1_q = {}
+        tab_codes = []
+
+        def w1_pass(a, b, start, stop):
+            codes, scales = w1_q[a, b]
+            for t in range(PACK):
+                cols = slice(t * P, (t + 1) * P)
+                nc.tensor.matmul_mx(
+                    out=sums[PACK * b + t][:], lhsT=codes[:, cols].bitcast(FP8X4), lhsT_scale=scales[:, cols],
+                    rhs=tab_codes[a][:].bitcast(FP8X4), rhs_scale=tab_planes[tab_row[a] :, :],
+                    start=start, stop=stop,
+                )
+
+        def w4_pass(b, stop):
+            for t in range(PACK):
+                c0 = b * K_PASS + t * P
+                nc.tensor.matmul_mx(
+                    out=sums[PACK * b + t][:], lhsT=w4_codes[:, 2 * c0 : 2 * (c0 + P)].bitcast(FP4X4),
+                    lhsT_scale=w4_planes[:, c0 : c0 + P],
+                    rhs=tab_codes[W1_PASSES][:].bitcast(FP8X4), rhs_scale=tab_planes[:],
+                    start=False, stop=stop,
+                )
+
+        def squash(b):
+            squashed = sb("squashed%d" % b, [P, PACK, S], F32)
+            for t in range(PACK):
+                nc.scalar.activation(squashed[:, t, :], sums[PACK * b + t][:], ACT.Tanh)
+            return squashed
+
+        def combine(b, squashed):
+            planar = sb("h_planar%d" % b, [P, PACK, S], BF16)
+            for t in range(PACK):
+                nc.vector.scalar_tensor_tensor(
+                    out=planar[:, t, :], in0=squashed[:, t, :], scalar=gain_sb[:, b, t : t + 1],
+                    in1=res_sb[b][:, t, :], op0=ALU.mult, op1=ALU.add,
+                )
+            grouped = sb("h_bf%d" % b, [P, S * PACK], BF16)
+            nc.scalar.copy(
+                grouped[:].rearrange("p (c i t) -> p c t i", i=NEAR, t=PACK),
+                planar[:].rearrange("p t (c i) -> p c t i", i=NEAR),
+            )
+            return grouped
+
+        tab_codes.append(gather_words("tab_codes0", tab_win[0], lists[0]))
+        w1_q[0, 0] = quantize("w1q00", round_w1(0, 0, P))
+        tab_planes = gather_scales("tab_planes", scale_win[0], lists[0])
+        w1_pass(0, 0, True, False)
+        tab_codes.append(gather_words("tab_codes1", tab_win[1], lists[0]))
+        w1_q[1, 0] = quantize("w1q10", round_w1(1, 0, P))
+        w1_pass(1, 0, False, False)
+
+        w4_codes = sb("w4_codes", [P, 2 * H], U8)
+        w4_planes = sb("w4_planes", [P, H], U8)
+        nc.vector.tensor_copy(
+            w4_codes[:].bitcast(U16).rearrange("p (b t m) -> p b m t", b=H_PASSES, t=PACK),
+            w4_raw[:].bitcast(U16).rearrange("p (b m t) -> p b m t", b=H_PASSES, t=PACK),
+        )
+        nc.vector.tensor_copy(
+            w4_planes[:].rearrange("p (b t m) -> p b m t", b=H_PASSES, t=PACK),
+            w4_scale_raw[:].rearrange("p (b m t) -> p b m t", b=H_PASSES, t=PACK),
+        )
+        tab_codes.append(gather_words("tab_codes2", tab_win[2], lists[0]))
+        w4_pass(0, True)
+        w1_q[0, 1] = quantize("w1q01", round_w1(0, 1, P))
+        squashed0 = squash(0)
+        w1_pass(0, 1, True, False)
+        w4_pass(1, False)
+        w1_q[1, 1] = quantize("w1q11", round_w1(1, 1, 0))
+        w1_pass(1, 1, False, True)
+        squashed1 = squash(1)
+        tab2_planes = gather_scales("tab2_planes", scale_win[1], lists[1])
+        grouped0 = combine(0, squashed0)
+        grouped1 = combine(1, squashed1)
+        tab3_planes = gather_scales("tab3_planes", scale_win[2], lists[2], "res1")
+        tab2_codes = [gather_words("tab2_codes0", tab2_win[0], lists[1])]
+        h_q = [quantize("hq0", grouped0, "tab2_win0"), quantize("hq1", grouped1)]
+        tab2_codes.append(gather_words("tab2_codes1", tab2_win[1], lists[1]))
+
+        def score_pass(acc, codes, planes, first_row, b, mt):
+            cols = slice(mt * P, (mt + 1) * P)
+            nc.tensor.matmul_mx(
+                out=acc[:], lhsT=codes[:, cols].bitcast(FP8X4), lhsT_scale=planes[first_row:, cols],
+                rhs=h_q[b][0][:].bitcast(FP8X4), rhs_scale=h_q[b][1][:],
+                start=(b == 0), stop=(b == H_PASSES - 1),
+            )
+
+        e2 = [bank(mt) for mt in range(M_TILES)]
+        for b in range(H_PASSES):
+            for mt in range(M_TILES):
+                score_pass(e2[mt], tab2_codes[b], tab2_planes, tab2_row[b], b, mt)
+        strength = []
+        for mt in range(M_TILES):
+            strength.append(sb("strength%d" % mt, [P, S], F32))
+            nc.scalar.activation(strength[mt][:], e2[mt][:], ACT.Abs)
+
+        e3 = [bank(M_TILES + mt) for mt in range(M_TILES)]
+        for b in range(H_PASSES):
+            pieces = M_TILES if b == H_PASSES - 1 else 1
+            codes = gather_words("tab3_codes%d" % b, tab3_win[b], lists[2], pieces)
+            for mt in range(M_TILES):
+                score_pass(e3[mt], codes, tab3_planes, tab3_row[b], b, mt)
+
+        for mt in range(M_TILES):
+            colour = sb("colour%d" % mt, [P, S], F32)
+            nc.scalar.activation(colour[:], e3[mt][:], ACT.Tanh)
+            product = sb("product%d" % mt, [P, S], F32)
+            nc.vector.tensor_tensor(product[:], e2[mt][:], colour[:], ALU.mult)
+            score = sb("score%d" % mt, [P, S], F32)
+            nc.vector.tensor_tensor(score[:], product[:], strength[mt][:], ALU.add)
+            nc.sync.dma_start(out=out[mt * P : (mt + 1) * P, :], in_=score[:])

@@ -45,15 +45,9 @@ def tile_list_board_longlist_readout_kernel(
             return psum.tile([P, S], F32, name="bank%d" % index)
 
         lists = [sb("list%d" % i, [P, LIST_COLS], U16) for i in range(3)]
-        tab_win = [sb("tab_win%d" % a, [P, T], I32) for a in range(3)]
-        tab2_win = [sb("tab2_win%d" % a, [P, T], I32) for a in range(H_PASSES)]
-        tab3_win = [sb("tab3_win%d" % a, [P, T], I32) for a in range(H_PASSES)]
         scale_win = [sb("scale_win%d" % i, [P, T], U8) for i in range(3)]
         w4_raw = sb("w4_raw", [P, 2 * H], U8)
         w4_scale_raw = sb("w4_scale_raw", [P, H], U8)
-        w1_raw = {(a, b): sb("w1_raw%d%d" % (a, b), [P, PACK, K_PASS], F32)
-                  for a in range(W1_PASSES) for b in range(H_PASSES)}
-        res_sb = [sb("res%d" % b, [P, PACK, S], F32) for b in range(H_PASSES)]
         gain_sb = sb("gain_sb", [P, H_PASSES, PACK], F32)
 
         for plane in (scale_win[0], w4_scale_raw, scale_win[1], scale_win[2]):
@@ -75,16 +69,22 @@ def tile_list_board_longlist_readout_kernel(
         tab2_row = (0, 4)
         tab3_row = (8, 12)
 
-        def load_words(win, words):
+        def load_words(name, words, reuse=None):
+            win = sb(name, [P, T], I32, reuse)
             nc.sync.dma_start(out=win[:], in_=words.rearrange("p t i -> p (t i)").bitcast(I32))
+            return win
 
-        def load_w1(a, b):
+        def load_w1(a, b, reuse=None):
+            raw = sb("w1_raw%d%d" % (a, b), [P, PACK, K_PASS], F32, reuse)
             rows = w1[a * K_PASS : (a + 1) * K_PASS, b * K_PASS : (b + 1) * K_PASS]
-            nc.sync.dma_start(out=w1_raw[a, b][:], in_=rows.rearrange("(p j) c -> p j c", j=PACK))
+            nc.sync.dma_start(out=raw[:], in_=rows.rearrange("(p j) c -> p j c", j=PACK))
+            return raw
 
-        def load_res(b):
+        def load_res(b, reuse):
+            res_sb = sb("res%d" % b, [P, PACK, S], F32, reuse)
             rows = res[b * K_PASS : (b + 1) * K_PASS, :]
-            nc.sync.dma_start(out=res_sb[b][:], in_=rows.rearrange("(p t) j -> p t j", t=PACK))
+            nc.sync.dma_start(out=res_sb[:], in_=rows.rearrange("(p t) j -> p t j", t=PACK))
+            return res_sb
 
         def load_w4():
             nc.sync.dma_start(out=w4_raw[:].bitcast(I32), in_=w4_words[0].bitcast(I32))
@@ -95,32 +95,36 @@ def tile_list_board_longlist_readout_kernel(
         def load_list(i, offsets):
             nc.sync.dma_start(lists[i][:], offsets)
 
-        large = [
-            partial(load_w1, 0, 0), partial(load_words, tab_win[0], tab_words[0]),
-            partial(load_w1, 1, 0), partial(load_words, tab_win[1], tab_words[1]),
-            partial(load_w1, 0, 1), partial(load_words, tab_win[2], tab_words[2]),
-            partial(load_w1, 1, 1), partial(load_res, 0), partial(load_res, 1),
-        ]
-        large.extend(partial(load_words, tab2_win[a], tab2_words[a]) for a in range(H_PASSES))
-        large.extend(partial(load_words, tab3_win[a], tab3_words[a]) for a in range(H_PASSES))
-        small = [partial(load_list, 0, offs)]
-        small.extend(scale_loads(nc.sync, scale_win[0], tab_row[0], tab_scales[0:W1_PASSES]))
-        small.extend(scale_loads(nc.sync, scale_win[0], tab_row[2], tab_scales[W1_PASSES : W1_PASSES + 1]))
-        small.append(load_w4)
-        small.extend(scale_loads(nc.sync, w4_scale_raw, 0, w4_scales))
-        small.append(partial(load_list, 1, offs2))
-        small.extend(scale_loads(nc.sync, scale_win[1], tab2_row[0], tab2_scales))
-        small.extend([load_gain, partial(load_list, 2, offs3)])
-        small.extend(scale_loads(nc.sync, scale_win[2], tab3_row[0], tab3_scales))
-        large[0]()
-        for i, load in enumerate(large[1:]):
+        for load in (
+            scale_loads(nc.gpsimd, scale_win[0], tab_row[0], tab_scales[0:W1_PASSES])
+            + scale_loads(nc.gpsimd, scale_win[1], tab2_row[0], tab2_scales)
+            + scale_loads(nc.gpsimd, scale_win[2], tab3_row[0], tab3_scales)
+        ):
             load()
-            first = 0 if i == 0 else 3 * (i + 1)
-            for small_load in small[first : 3 * (i + 2)]:
-                small_load()
+        board_scales = scale_loads(nc.sync, scale_win[0], tab_row[2], tab_scales[W1_PASSES : W1_PASSES + 1])
+        w4_scale_loads = scale_loads(nc.sync, w4_scale_raw, 0, w4_scales)
 
-        def gather_words(name, win, offsets, pieces=1):
-            picked = sb(name, [P, S], U32)
+        raw00 = load_w1(0, 0)
+        tab_win0 = load_words("tab_win0", tab_words[0])
+        load_list(0, offs)
+        board_scales[0]()
+        board_scales[1]()
+        raw10 = load_w1(1, 0)
+        board_scales[2]()
+        board_scales[3]()
+        tab_win1 = load_words("tab_win1", tab_words[1])
+        load_w4()
+        w4_scale_loads[0]()
+        w4_scale_loads[1]()
+        raw01 = load_w1(0, 1)
+        w4_scale_loads[2]()
+        w4_scale_loads[3]()
+        load_list(1, offs2)
+        load_gain()
+        load_list(2, offs3)
+
+        def gather_words(name, win, offsets, reuse=None, pieces=1):
+            picked = sb(name, [P, S], U32, reuse)
             width = S // pieces
             for i in range(pieces):
                 piece = offsets[:, i * width // 16 : (i + 1) * width // 16]
@@ -132,10 +136,10 @@ def tile_list_board_longlist_readout_kernel(
             nc.vector.tensor_copy(picked[:], win[:].indirect(offsets[:]))
             return picked
 
-        def round_w1(a, b, scalar_share):
-            grouped = sb("w1_bf%d%d" % (a, b), [P, PACK * K_PASS], BF16)
+        def round_w1(name, raw, scalar_share, reuse=None):
+            grouped = sb(name, [P, PACK * K_PASS], BF16, reuse)
             dst = grouped[:].rearrange("p (t m j) -> p m j t", t=PACK, j=PACK)
-            src = w1_raw[a, b][:].rearrange("p j (m t) -> p m j t", t=PACK)
+            src = raw[:].rearrange("p j (m t) -> p m j t", t=PACK)
             if scalar_share > 0:
                 nc.scalar.copy(dst[:, :scalar_share], src[:, :scalar_share])
             if scalar_share < P:
@@ -178,12 +182,12 @@ def tile_list_board_longlist_readout_kernel(
                 nc.scalar.activation(squashed[:, t, :], sums[PACK * b + t][:], ACT.Tanh)
             return squashed
 
-        def combine(b, squashed):
-            planar = sb("h_planar%d" % b, [P, PACK, S], BF16)
+        def combine(b, squashed, res_sb, reuse=None):
+            planar = sb("h_planar%d" % b, [P, PACK, S], BF16, reuse)
             for t in range(PACK):
                 nc.vector.scalar_tensor_tensor(
                     out=planar[:, t, :], in0=squashed[:, t, :], scalar=gain_sb[:, b, t : t + 1],
-                    in1=res_sb[b][:, t, :], op0=ALU.mult, op1=ALU.add,
+                    in1=res_sb[:, t, :], op0=ALU.mult, op1=ALU.add,
                 )
             grouped = sb("h_bf%d" % b, [P, S * PACK], BF16)
             nc.scalar.copy(
@@ -192,12 +196,16 @@ def tile_list_board_longlist_readout_kernel(
             )
             return grouped
 
-        tab_codes.append(gather_words("tab_codes0", tab_win[0], lists[0]))
-        w1_q[0, 0] = quantize("w1q00", round_w1(0, 0, P))
+        tab_codes.append(gather_words("tab_codes0", tab_win0, lists[0]))
+        w1_q[0, 0] = quantize("w1q00", round_w1("w1_bf00", raw00, P))
+        tab_win2 = load_words("tab_win2", tab_words[2], "w1_raw00")
+        raw11 = load_w1(1, 1, "tab_win0")
         tab_planes = gather_scales("tab_planes", scale_win[0], lists[0])
         w1_pass(0, 0, True, False)
-        tab_codes.append(gather_words("tab_codes1", tab_win[1], lists[0]))
-        w1_q[1, 0] = quantize("w1q10", round_w1(1, 0, P))
+        tab_codes.append(gather_words("tab_codes1", tab_win1, lists[0]))
+        w1_q[1, 0] = quantize("w1q10", round_w1("w1_bf10", raw10, P))
+        res0 = load_res(0, "w1_raw10")
+        res1 = load_res(1, "tab_win1")
         w1_pass(1, 0, False, False)
 
         w4_codes = sb("w4_codes", [P, 2 * H], U8)
@@ -210,22 +218,29 @@ def tile_list_board_longlist_readout_kernel(
             w4_planes[:].rearrange("p (b t m) -> p b m t", b=H_PASSES, t=PACK),
             w4_scale_raw[:].rearrange("p (b m t) -> p b m t", b=H_PASSES, t=PACK),
         )
-        tab_codes.append(gather_words("tab_codes2", tab_win[2], lists[0]))
+        tab2_planes = gather_scales("tab2_planes", scale_win[1], lists[1])
+        tab_codes.append(gather_words("tab_codes2", tab_win2, lists[0]))
         w4_pass(0, True)
-        w1_q[0, 1] = quantize("w1q01", round_w1(0, 1, P))
+        w1_q[0, 1] = quantize("w1q01", round_w1("w1_bf01", raw01, P), "scale_win1")
+        tab2_win0 = load_words("tab2_win0", tab2_words[0], "w1_raw01")
+        tab2_win1 = load_words("tab2_win1", tab2_words[1], "w1_raw00")
         squashed0 = squash(0)
         w1_pass(0, 1, True, False)
         w4_pass(1, False)
-        w1_q[1, 1] = quantize("w1q11", round_w1(1, 1, 0))
+        tab3_planes = gather_scales("tab3_planes", scale_win[2], lists[2])
+        w1_q[1, 1] = quantize("w1q11", round_w1("w1_bf11", raw11, 0, "scale_win2"))
+        tab3_win0 = load_words("tab3_win0", tab3_words[0], "tab_win0")
         w1_pass(1, 1, False, True)
         squashed1 = squash(1)
-        tab2_planes = gather_scales("tab2_planes", scale_win[1], lists[1])
-        grouped0 = combine(0, squashed0)
-        grouped1 = combine(1, squashed1)
-        tab3_planes = gather_scales("tab3_planes", scale_win[2], lists[2], "res1")
-        tab2_codes = [gather_words("tab2_codes0", tab2_win[0], lists[1])]
-        h_q = [quantize("hq0", grouped0, "tab2_win0"), quantize("hq1", grouped1)]
-        tab2_codes.append(gather_words("tab2_codes1", tab2_win[1], lists[1]))
+        grouped0 = combine(0, squashed0, res0, "scale_win2")
+        tab3_win1 = load_words("tab3_win1", tab3_words[1], "w1_raw10")
+        grouped1 = combine(1, squashed1, res1)
+        tab2_codes = [gather_words("tab2_codes0", tab2_win0, lists[1], "tab_win1")]
+        h_q = [quantize("hq0", grouped0, "w1_raw01")]
+        tab2_codes.append(gather_words("tab2_codes1", tab2_win1, lists[1], "h_bf0"))
+        h_q.append(quantize("hq1", grouped1, "w1_raw00"))
+        tab3_codes = [gather_words("tab3_codes0", tab3_win0, lists[2], "h_bf1")]
+        tab3_codes.append(gather_words("tab3_codes1", tab3_win1, lists[2], "tab_win0", M_TILES))
 
         def score_pass(acc, codes, planes, first_row, b, mt):
             cols = slice(mt * P, (mt + 1) * P)
@@ -246,10 +261,8 @@ def tile_list_board_longlist_readout_kernel(
 
         e3 = [bank(M_TILES + mt) for mt in range(M_TILES)]
         for b in range(H_PASSES):
-            pieces = M_TILES if b == H_PASSES - 1 else 1
-            codes = gather_words("tab3_codes%d" % b, tab3_win[b], lists[2], pieces)
             for mt in range(M_TILES):
-                score_pass(e3[mt], codes, tab3_planes, tab3_row[b], b, mt)
+                score_pass(e3[mt], tab3_codes[b], tab3_planes, tab3_row[b], b, mt)
 
         for mt in range(M_TILES):
             colour = sb("colour%d" % mt, [P, S], F32)

from contextlib import ExitStack
from functools import partial

import concourse.mybir as mybir

K, KA, KB, H, T, S = 1536, 1024, 512, 1024, 2048, 512
FLOPS = 2 * K * H * S + 2 * 2 * H * S * S

F32 = mybir.dt.float32
BF16 = mybir.dt.bfloat16
I32 = mybir.dt.int32
U32 = mybir.dt.uint32
U16 = mybir.dt.uint16
U8 = mybir.dt.uint8
FP8X4 = mybir.dt.float8_e4m3fn_x4
FP4X4 = mybir.dt.float4_e2m1fn_x4
ACT = mybir.ActivationFunctionType
ALU = mybir.AluOpType

P = 128
PACK = 4
K_PASS = P * PACK
QUADS = 4
QUAD = P // QUADS
H_PASSES = H // K_PASS
W1_PASSES = KA // K_PASS
M_TILES = S // P
LIST_COLS = S // 16
NEAR = 4


def tile_list_board_longlist_readout_kernel(
    tc, tab_words, tab_scales, offs, w1, w4_words, w4_scales, gain, res,
    tab2_words, tab2_scales, offs2, tab3_words, tab3_scales, offs3, out,
):
    nc = tc.nc
    with ExitStack() as ctx:
        keep = ctx.enter_context(tc.tile_pool(name="keep", bufs=1))
        psum = ctx.enter_context(tc.psum_pool(name="psum", bufs=1))

        def sb(name, shape, dtype, reuse=None):
            return keep.tile(shape, dtype, name=name, tag=reuse or name, align_bytes=64)

        def bank(index):
            return psum.tile([P, S], F32, name="bank%d" % index)

        lists = [sb("list%d" % i, [P, LIST_COLS], U16) for i in range(3)]
        scale_win = [sb("scale_win%d" % i, [P, T], U8) for i in range(3)]
        w4_raw = sb("w4_raw", [P, 2 * H], U8)
        w4_scale_raw = sb("w4_scale_raw", [P, H], U8)
        gain_sb = sb("gain_sb", [P, H_PASSES, PACK], F32)

        for plane in (scale_win[0], w4_scale_raw, scale_win[1], scale_win[2]):
            nc.vector.memset(plane[:].bitcast(I32), 0)

        def scale_loads(engine, plane, first_row, scales):
            rows = scales.shape[0] * PACK

            def load(q):
                p0 = QUAD * q + first_row
                engine.dma_start(
                    out=plane[p0 : p0 + rows, :].bitcast(I32),
                    in_=scales[:, PACK * q : PACK * (q + 1), :].bitcast(I32),
                )

            return [partial(load, q) for q in range(QUADS)]

        tab_row = (4, 8, 0)
        tab2_row = (0, 4)
        tab3_row = (8, 12)

        def load_words(name, words, reuse=None):
            win = sb(name, [P, T], I32, reuse)
            nc.sync.dma_start(out=win[:], in_=words.rearrange("p t i -> p (t i)").bitcast(I32))
            return win

        def load_w1(a, b, reuse=None):
            raw = sb("w1_raw%d%d" % (a, b), [P, PACK, K_PASS], F32, reuse)
            rows = w1[a * K_PASS : (a + 1) * K_PASS, b * K_PASS : (b + 1) * K_PASS]
            nc.sync.dma_start(out=raw[:], in_=rows.rearrange("(p j) c -> p j c", j=PACK))
            return raw

        def load_res(b, reuse):
            res_sb = sb("res%d" % b, [P, PACK, S], F32, reuse)
            rows = res[b * K_PASS : (b + 1) * K_PASS, :]
            nc.sync.dma_start(out=res_sb[:], in_=rows.rearrange("(p t) j -> p t j", t=PACK))
            return res_sb

        def load_w4():
            nc.sync.dma_start(out=w4_raw[:].bitcast(I32), in_=w4_words[0].bitcast(I32))

        def load_gain():
            nc.sync.dma_start(out=gain_sb[:], in_=gain.rearrange("(b p t) -> p b t", p=P, t=PACK))

        def load_list(i, offsets):
            nc.sync.dma_start(lists[i][:], offsets)

        for load in (
            scale_loads(nc.gpsimd, scale_win[0], tab_row[0], tab_scales[0:W1_PASSES])
            + scale_loads(nc.gpsimd, scale_win[1], tab2_row[0], tab2_scales)
            + scale_loads(nc.gpsimd, scale_win[2], tab3_row[0], tab3_scales)
        ):
            load()
        board_scales = scale_loads(nc.sync, scale_win[0], tab_row[2], tab_scales[W1_PASSES : W1_PASSES + 1])
        w4_scale_loads = scale_loads(nc.sync, w4_scale_raw, 0, w4_scales)

        raw00 = load_w1(0, 0)
        tab_win0 = load_words("tab_win0", tab_words[0])
        load_list(0, offs)
        board_scales[0]()
        board_scales[1]()
        raw10 = load_w1(1, 0)
        board_scales[2]()
        board_scales[3]()
        tab_win1 = load_words("tab_win1", tab_words[1])
        load_w4()
        w4_scale_loads[0]()
        w4_scale_loads[1]()
        raw01 = load_w1(0, 1)
        w4_scale_loads[2]()
        w4_scale_loads[3]()
        load_list(1, offs2)
        load_gain()
        load_list(2, offs3)

        def gather_words(name, win, offsets, reuse=None, pieces=1):
            picked = sb(name, [P, S], U32, reuse)
            width = S // pieces
            for i in range(pieces):
                piece = offsets[:, i * width // 16 : (i + 1) * width // 16]
                nc.vector.tensor_copy(picked[:, i * width : (i + 1) * width], win[:].bitcast(U32).indirect(piece))
            return picked

        def gather_scales(name, win, offsets, reuse=None):
            picked = sb(name, [P, S], U8, reuse)
            nc.vector.tensor_copy(picked[:], win[:].indirect(offsets[:]))
            return picked

        def round_w1(name, raw, scalar_share, reuse=None):
            grouped = sb(name, [P, PACK * K_PASS], BF16, reuse)
            dst = grouped[:].rearrange("p (t m j) -> p m j t", t=PACK, j=PACK)
            src = raw[:].rearrange("p j (m t) -> p m j t", t=PACK)
            if scalar_share > 0:
                nc.scalar.copy(dst[:, :scalar_share], src[:, :scalar_share])
            if scalar_share < P:
                nc.vector.tensor_copy(dst[:, scalar_share:], src[:, scalar_share:])
            return grouped

        def quantize(name, grouped, reuse=None):
            codes = sb(name + "_codes", [P, K_PASS], U32, reuse)
            scales = sb(name + "_scales", [P, K_PASS], U8)
            nc.vector.quantize_mx(out=codes[:].bitcast(FP8X4), scales=scales[:], in_=grouped[:])
            return codes, scales

        sums = [bank(i) for i in range(H_PASSES * PACK)]
        w1_q = {}
        tab_codes = []

        def w1_pass(a, b, start, stop):
            codes, scales = w1_q[a, b]
            for t in range(PACK):
                cols = slice(t * P, (t + 1) * P)
                nc.tensor.matmul_mx(
                    out=sums[PACK * b + t][:], lhsT=codes[:, cols].bitcast(FP8X4), lhsT_scale=scales[:, cols],
                    rhs=tab_codes[a][:].bitcast(FP8X4), rhs_scale=tab_planes[tab_row[a] :, :],
                    start=start, stop=stop,
                )

        def w4_pass(b, stop):
            for t in range(PACK):
                c0 = b * K_PASS + t * P
                nc.tensor.matmul_mx(
                    out=sums[PACK * b + t][:], lhsT=w4_codes[:, 2 * c0 : 2 * (c0 + P)].bitcast(FP4X4),
                    lhsT_scale=w4_planes[:, c0 : c0 + P],
                    rhs=tab_codes[W1_PASSES][:].bitcast(FP8X4), rhs_scale=tab_planes[:],
                    start=False, stop=stop,
                )

        def squash(b):
            squashed = sb("squashed%d" % b, [P, PACK, S], F32)
            for t in range(PACK):
                nc.scalar.activation(squashed[:, t, :], sums[PACK * b + t][:], ACT.Tanh)
            return squashed

        def combine(b, squashed, res_sb, reuse=None):
            planar = sb("h_planar%d" % b, [P, PACK, S], BF16, reuse)
            for t in range(PACK):
                nc.vector.scalar_tensor_tensor(
                    out=planar[:, t, :], in0=squashed[:, t, :], scalar=gain_sb[:, b, t : t + 1],
                    in1=res_sb[:, t, :], op0=ALU.mult, op1=ALU.add,
                )
            grouped = sb("h_bf%d" % b, [P, S * PACK], BF16)
            nc.scalar.copy(
                grouped[:].rearrange("p (c i t) -> p c t i", i=NEAR, t=PACK),
                planar[:].rearrange("p t (c i) -> p c t i", i=NEAR),
            )
            return grouped

        tab_codes.append(gather_words("tab_codes0", tab_win0, lists[0]))
        w1_q[0, 0] = quantize("w1q00", round_w1("w1_bf00", raw00, P))
        tab_win2 = load_words("tab_win2", tab_words[2], "w1_raw00")
        raw11 = load_w1(1, 1, "tab_win0")
        tab_planes = gather_scales("tab_planes", scale_win[0], lists[0])
        w1_pass(0, 0, True, False)
        tab_codes.append(gather_words("tab_codes1", tab_win1, lists[0]))
        w1_q[1, 0] = quantize("w1q10", round_w1("w1_bf10", raw10, P))
        res0 = load_res(0, "w1_raw10")
        res1 = load_res(1, "tab_win1")
        w1_pass(1, 0, False, False)

        w4_codes = sb("w4_codes", [P, 2 * H], U8)
        w4_planes = sb("w4_planes", [P, H], U8)
        nc.vector.tensor_copy(
            w4_codes[:].bitcast(U16).rearrange("p (b t m) -> p b m t", b=H_PASSES, t=PACK),
            w4_raw[:].bitcast(U16).rearrange("p (b m t) -> p b m t", b=H_PASSES, t=PACK),
        )
        nc.vector.tensor_copy(
            w4_planes[:].rearrange("p (b t m) -> p b m t", b=H_PASSES, t=PACK),
            w4_scale_raw[:].rearrange("p (b m t) -> p b m t", b=H_PASSES, t=PACK),
        )
        tab2_planes = gather_scales("tab2_planes", scale_win[1], lists[1])
        tab_codes.append(gather_words("tab_codes2", tab_win2, lists[0]))
        w4_pass(0, True)
        w1_q[0, 1] = quantize("w1q01", round_w1("w1_bf01", raw01, P), "scale_win1")
        tab2_win0 = load_words("tab2_win0", tab2_words[0], "w1_raw01")
        tab2_win1 = load_words("tab2_win1", tab2_words[1], "w1_raw00")
        squashed0 = squash(0)
        w1_pass(0, 1, True, False)
        w4_pass(1, False)
        tab3_planes = gather_scales("tab3_planes", scale_win[2], lists[2])
        w1_q[1, 1] = quantize("w1q11", round_w1("w1_bf11", raw11, 0, "scale_win2"))
        tab3_win0 = load_words("tab3_win0", tab3_words[0], "tab_win0")
        w1_pass(1, 1, False, True)
        squashed1 = squash(1)
        grouped0 = combine(0, squashed0, res0, "scale_win2")
        tab3_win1 = load_words("tab3_win1", tab3_words[1], "w1_raw10")
        grouped1 = combine(1, squashed1, res1)
        tab2_codes = [gather_words("tab2_codes0", tab2_win0, lists[1], "tab_win1")]
        h_q = [quantize("hq0", grouped0, "w1_raw01")]
        tab2_codes.append(gather_words("tab2_codes1", tab2_win1, lists[1], "h_bf0"))
        h_q.append(quantize("hq1", grouped1, "w1_raw00"))
        tab3_codes = [gather_words("tab3_codes0", tab3_win0, lists[2], "h_bf1")]
        tab3_codes.append(gather_words("tab3_codes1", tab3_win1, lists[2], "tab_win0", M_TILES))

        def score_pass(acc, codes, planes, first_row, b, mt):
            cols = slice(mt * P, (mt + 1) * P)
            nc.tensor.matmul_mx(
                out=acc[:], lhsT=codes[:, cols].bitcast(FP8X4), lhsT_scale=planes[first_row:, cols],
                rhs=h_q[b][0][:].bitcast(FP8X4), rhs_scale=h_q[b][1][:],
                start=(b == 0), stop=(b == H_PASSES - 1),
            )

        e2 = [bank(mt) for mt in range(M_TILES)]
        for b in range(H_PASSES):
            for mt in range(M_TILES):
                score_pass(e2[mt], tab2_codes[b], tab2_planes, tab2_row[b], b, mt)
        strength = []
        for mt in range(M_TILES):
            strength.append(sb("strength%d" % mt, [P, S], F32))
            nc.scalar.activation(strength[mt][:], e2[mt][:], ACT.Abs)

        e3 = [bank(M_TILES + mt) for mt in range(M_TILES)]
        for b in range(H_PASSES):
            for mt in range(M_TILES):
                score_pass(e3[mt], tab3_codes[b], tab3_planes, tab3_row[b], b, mt)

        for mt in range(M_TILES):
            colour = sb("colour%d" % mt, [P, S], F32)
            nc.scalar.activation(colour[:], e3[mt][:], ACT.Tanh)
            product = sb("product%d" % mt, [P, S], F32)
            nc.vector.tensor_tensor(product[:], e2[mt][:], colour[:], ALU.mult)
            score = sb("score%d" % mt, [P, S], F32)
            nc.vector.tensor_tensor(score[:], product[:], strength[mt][:], ALU.add)
            nc.sync.dma_start(out=out[mt * P : (mt + 1) * P, :], in_=score[:])
